import numpy as np
import ml_dtypes


def mxq(x, axis, fmt="e4m3"):
    dtype, down = {"e4m3": (ml_dtypes.float8_e4m3fn, 7), "e5m2": (ml_dtypes.float8_e5m2, 14)}[fmt]
    v = np.moveaxis(np.asarray(x, np.float32).astype(ml_dtypes.bfloat16).astype(np.float64), axis, -1)
    blocks = v.reshape(v.shape[:-1] + (-1, 32))
    amax = np.abs(blocks).max(-1, keepdims=True)
    byte = np.maximum(np.where(amax > 0, np.frexp(amax)[1] - 1 + 127, 0) - down, 1)
    scale = np.exp2(byte - 127.0)
    codes = (blocks / scale).astype(np.float32).astype(dtype).astype(np.float64)
    return np.moveaxis((codes * scale).reshape(v.shape), -1, axis)


WIDE = False


def mx_kscale(k):
    if not WIDE:
        return np.ones(k)
    levels = np.array([10, -10, 5, -5, 0])
    if k % 512:
        return np.exp2(np.random.permutation(np.resize(levels, k // 32))).repeat(32)
    a = np.empty((k // 512, 16))
    for p in range(k // 512):
        a[p, :8] = np.random.permutation(np.resize(levels, 8))
        for g in range(8):
            far = levels[np.abs(levels - a[p, g]) >= 10]
            a[p, g + 8] = far[np.random.randint(len(far))]
    return np.exp2(a.ravel()).repeat(32)


BF16 = ml_dtypes.bfloat16


def bf(x):
    return np.asarray(x, np.float32).astype(BF16)


def f64(x):
    return np.asarray(x).astype(np.float64)


N, K, P, H = 8192, 512, 512, 128


def draw0():
    s = mx_kscale(K)
    r = mx_kscale(P)
    t = mx_kscale(P)
    return {
        "z": bf(np.random.standard_normal((N, K)) * s),
        "m": bf(np.random.standard_normal((N, P)) * r),
        "ez": bf(np.random.standard_normal(K) / np.sqrt(K) / s),
        "at": bf(np.random.standard_normal((P, P)) / np.sqrt(P) / r[:, None] * t),
        "bvec": bf(np.random.standard_normal(P) * 0.7 * t),
        "wz": bf(np.random.standard_normal((K, H)) * 0.7 / np.sqrt(K) / s[:, None]),
        "wm": bf(np.random.standard_normal((P, H)) * 0.7 / np.sqrt(P) / t[:, None]),
    }


def write_scalar(z, ez):
    return np.sum(z * ez[None, :], axis=-1)


def update_memory(m, u, at, bvec):
    a = mxq(m, 1, "e4m3") @ mxq(at, 0, "e4m3")
    return a + u[:, None] * bvec[None, :]


def core(z, m, ez, at, bvec, wz, wm):
    z, m = f64(z), f64(m)
    u = write_scalar(z, f64(ez))
    m_new = update_memory(m, u, f64(at), f64(bvec))
    s = (mxq(z, 1, "e4m3") @ mxq(f64(wz), 0, "e4m3")) + (mxq(m_new, 1, "e4m3") @ mxq(f64(wm), 0, "e4m3"))
    return np.tanh(s)


def e4m3fn_bytes(y):
    return np.clip(np.asarray(y, np.float64), -448.0, 448.0).astype(np.float32).astype(ml_dtypes.float8_e4m3fn).view(np.uint8)


def e4m3fn_values(b):
    return np.asarray(b, np.uint8).view(ml_dtypes.float8_e4m3fn).astype(np.float64)


def setup_inputs():
    d = draw0()
    x0 = np.asarray(d['m']).astype(np.float64)
    s = (np.max(np.abs(x0), axis=(0,), keepdims=True) / 448.0).astype(np.float32)
    out = {}
    for k, v in d.items():
        if k == 'm':
            out['m_bytes'] = e4m3fn_bytes(x0 / s.astype(np.float64))
            out['m_scale'] = s
        else:
            out[k] = v
    return out


def reference(z, m_bytes, m_scale, ez, at, bvec, wz, wm):
    return core(z, e4m3fn_values(m_bytes) * m_scale.astype(np.float64), ez, at, bvec, wz, wm)

@@ -1,0 +1,259 @@
+from contextlib import ExitStack
+
+import concourse.mybir as mybir
+from concourse.masks import make_identity
+
+F32 = mybir.dt.float32
+BF16 = mybir.dt.bfloat16
+U32 = mybir.dt.uint32
+U8 = mybir.dt.uint8
+FP8 = mybir.dt.float8_e4m3fn
+FP8X4 = mybir.dt.float8_e4m3fn_x4
+ALU = mybir.AluOpType
+ACT = mybir.ActivationFunctionType
+
+P = 128
+N, K, C, H = 8192, 512, 512, 128
+TILES = 4
+GROUP = P * TILES
+GROUPS = N // GROUP
+FLOPS = 2 * N * K * (C + H + H)
+
+
+def tile_legendrememoryunitstep_t_kernel(tc, z, m_bytes, m_scale, ez, at, bvec, wz, wm, out):
+    nc = tc.nc
+    with ExitStack() as ctx:
+        keep = ctx.enter_context(tc.tile_pool(name="keep", bufs=1))
+        loads = ctx.enter_context(tc.tile_pool(name="loads", bufs=4))
+        work = ctx.enter_context(tc.tile_pool(name="work", bufs=3))
+        quant = ctx.enter_context(tc.tile_pool(name="quant", bufs=3))
+        turn = ctx.enter_context(tc.psum_pool(name="turn", bufs=3))
+        acc_pool = ctx.enter_context(tc.psum_pool(name="acc", bufs=4))
+        out_pool = ctx.enter_context(tc.psum_pool(name="outp", bufs=1))
+
+        z_view = z.rearrange("(g n i) k -> g n i k", n=P, i=TILES)
+        m_view = m_bytes.rearrange("(g n i) k -> g n i k", n=P, i=TILES)
+        out_view = out.rearrange("(g n i) h -> g n i h", n=P, i=TILES)
+
+        z_rows, m_rows, m_vals, z_grp, m_grp, n_rows, n_grp = {}, {}, {}, {}, {}, {}, {}
+        z_q, m_q, n_q, accs, u_cols = {}, {}, {}, {}, {}
+
+        def load_m(g, parts=1):
+            if not 0 <= g < GROUPS:
+                return
+            m_rows[g] = loads.tile([P, TILES, K], U8, name="m_rows", align_bytes=64)
+            w = TILES // parts
+            for q in range(parts):
+                nc.sync.dma_start(out=m_rows[g][:, w * q : w * (q + 1)], in_=m_view[g][:, w * q : w * (q + 1)])
+
+        def load_z(g):
+            if not 0 <= g < GROUPS:
+                return
+            z_rows[g] = loads.tile([P, TILES, K], BF16, name="z_rows", align_bytes=64)
+            nc.sync.dma_start(out=z_rows[g][:], in_=z_view[g])
+
+        with tc.manual_schedule():
+            scale_row = keep.tile([P, TILES, K], F32, name="scale_row", align_bytes=64)
+            nc.scalar.dma_start(out=scale_row[:, 0, :], in_=m_scale.rearrange("o k -> (o k)").partition_broadcast(P))
+            load_m(0, 2)
+            dummy = keep.tile([P, 1], F32, name="dummy")
+            nc.vector.memset(dummy[:], 0.0)
+            nc.scalar.activation(dummy[:], dummy[:], ACT.Tanh)
+            ident = keep.tile([P, P], F32, name="ident")
+            make_identity(nc, ident[:])
+            at_raw = keep.tile([P, 4, C], BF16, name="at_raw", align_bytes=64)
+            nc.sync.dma_start(out=at_raw[:], in_=at.rearrange("(p j) c -> p j c", j=4))
+            load_m(1)
+            load_z(0)
+            w_raw = keep.tile([P, 2, 4, H], BF16, name="w_raw", align_bytes=64)
+            nc.sync.dma_start(out=w_raw[:, 0], in_=wz.rearrange("(p j) h -> p j h", j=4))
+            nc.sync.dma_start(out=w_raw[:, 1], in_=wm.rearrange("(p j) h -> p j h", j=4))
+            ez_cols = keep.tile([P, 4], BF16, name="ez_cols")
+            nc.sync.dma_start(out=ez_cols[:], in_=ez.rearrange("(p t) -> p t", t=4))
+            load_z(1)
+            b_raw = keep.tile([P, C], BF16, name="b_raw", align_bytes=64)
+            nc.sync.dma_start(out=b_raw[:], in_=bvec.partition_broadcast(P))
+            for g in (2, 3):
+                load_m(g)
+                load_z(g)
+
+            b_row = keep.tile([P, C], BF16, name="b_row", align_bytes=64)
+            at_grp = keep.tile([P, C, 4], BF16, name="at_grp", align_bytes=64)
+            w_grp = keep.tile([P, 2, H, 4], BF16, name="w_grp", align_bytes=64)
+            at_codes = keep.tile([P, C], U32, name="at_codes", align_bytes=64)
+            at_scales = keep.tile([P, C], U8, name="at_scales", align_bytes=64)
+            w_codes = keep.tile([P, 2 * H], U32, name="w_codes", align_bytes=64)
+            w_scales = keep.tile([P, 2 * H], U8, name="w_scales", align_bytes=64)
+
+            def scale_m(g, parts=1):
+                if not 0 <= g < GROUPS:
+                    return
+                m_vals[g] = work.tile([P, TILES, K], BF16, name="m_vals", align_bytes=64)
+                w = TILES // parts
+                for q in range(parts):
+                    nc.vector.tensor_tensor(
+                        out=m_vals[g][:, w * q : w * (q + 1)].rearrange("p i k -> p (i k)"),
+                        in0=m_rows[g][:, w * q : w * (q + 1)].rearrange("p i k -> p (i k)").bitcast(FP8),
+                        in1=scale_row[:, :w].rearrange("p i k -> p (i k)"),
+                        op=ALU.mult,
+                    )
+
+            def turn_pair(rows, grp, b, step):
+                bank = turn.tile([P, 2, 2, P], F32, name="bank")
+                for i in range(2):
+                    words = rows[:, 2 * b + i, :].bitcast(F32)
+                    for u in range(2):
+                        src = words[:, u::2] if step == 2 else words[:, P * u : P * (u + 1)]
+                        nc.tensor.transpose(bank[:, i, u, :], src, ident[:])
+                dst = grp[:, 2 * P * b : 2 * P * (b + 1), :].rearrange("p n t -> p (n t)").bitcast(F32)
+                nc.scalar.copy(
+                    dst.rearrange("p (i n u) -> p i n u", i=2, u=2),
+                    bank[:].rearrange("p i u n -> p i n u"),
+                )
+
+            def turn_m(g):
+                if not 0 <= g < GROUPS:
+                    return
+                m_grp[g] = work.tile([P, GROUP, 4], BF16, name="m_grp", align_bytes=64)
+                for b in range(2):
+                    turn_pair(m_vals[g], m_grp[g], b, 2)
+
+            def turn_z(g):
+                if not 0 <= g < GROUPS:
+                    return
+                z_grp[g] = work.tile([P, GROUP, 4], BF16, name="z_grp", align_bytes=64)
+                for b in range(2):
+                    turn_pair(z_rows[g], z_grp[g], b, 2)
+
+            def quantize(grp, table, g, tag, parts=1):
+                if not 0 <= g < GROUPS:
+                    return
+                codes = quant.tile([P, GROUP], U32, name=tag + "_codes", align_bytes=64)
+                scales = quant.tile([P, GROUP], U8, name=tag + "_scales", align_bytes=64)
+                w = GROUP // parts
+                for q in range(parts):
+                    cols = slice(w * q, w * (q + 1))
+                    nc.vector.quantize_mx(
+                        out=codes[:, cols].bitcast(FP8X4),
+                        scales=scales[:, cols],
+                        in_=grp[:, cols, :].rearrange("p n t -> p (n t)"),
+                    )
+                table[g] = (codes, scales)
+
+            def mx(dst, left, cols, right, rcols, start, stop):
+                nc.tensor.matmul_mx(
+                    out=dst,
+                    lhsT=left[0][:, cols].bitcast(FP8X4),
+                    lhsT_scale=left[1][:, cols],
+                    rhs=right[0][:, rcols].bitcast(FP8X4),
+                    rhs_scale=right[1][:, rcols],
+                    start=start,
+                    stop=stop,
+                )
+
+            def finish(g, parts=1):
+                if not 0 <= g < GROUPS:
+                    return
+                res = out_pool.tile([P, TILES, H], F32, name="res")
+                o_rows = work.tile([P, TILES, H], F32, name="o_rows", align_bytes=64)
+                w = TILES // parts
+                for q in range(parts):
+                    for i in range(w * q, w * (q + 1)):
+                        cols = slice(P * i, P * (i + 1))
+                        mx(res[:, i, :], z_q[g], cols, (w_codes, w_scales), slice(0, H), True, False)
+                        mx(res[:, i, :], n_q[g], cols, (w_codes, w_scales), slice(H, 2 * H), False, True)
+                    part = slice(w * q, w * (q + 1))
+                    nc.scalar.activation(o_rows[:, part], res[:, part], ACT.Tanh)
+                    nc.sync.dma_start(out=out_view[g][:, part], in_=o_rows[:, part])
+
+            def write_scalar(g):
+                if not 0 <= g < GROUPS:
+                    return
+                u_bank = turn.tile([P, TILES], F32, name="bank")
+                for i in range(TILES):
+                    for t in range(4):
+                        nc.tensor.matmul(
+                            u_bank[:, i : i + 1],
+                            lhsT=z_grp[g][:, P * i : P * (i + 1), t],
+                            rhs=ez_cols[:, t : t + 1],
+                            start=(t == 0),
+                            stop=(t == 3),
+                        )
+                u_cols[g] = work.tile([P, TILES], F32, name="u_cols")
+                nc.scalar.copy(u_cols[g][:], u_bank[:])
+
+            def add_write(g):
+                if not 0 <= g < GROUPS:
+                    return
+                n_rows[g] = work.tile([P, TILES, C], BF16, name="n_rows", align_bytes=64)
+                n_grp[g] = work.tile([P, GROUP, 4], BF16, name="n_grp", align_bytes=64)
+                for b in range(2):
+                    for i in (2 * b, 2 * b + 1):
+                        nc.vector.scalar_tensor_tensor(
+                            out=n_rows[g][:, i, :],
+                            in0=b_row[:],
+                            scalar=u_cols[g][:, i : i + 1],
+                            in1=accs[g][i][:],
+                            op0=ALU.mult,
+                            op1=ALU.add,
+                        )
+                    turn_pair(n_rows[g], n_grp[g], b, 1)
+
+            def transition(g):
+                if not 0 <= g < GROUPS:
+                    return
+                accs[g] = []
+                for i in range(TILES):
+                    acc = acc_pool.tile([P, C], F32, name="acc")
+                    mx(acc[:], m_q[g], slice(P * i, P * (i + 1)), (at_codes, at_scales), slice(0, C), True, True)
+                    accs[g].append(acc)
+
+            def step(s):
+                last = GROUPS - 1
+                load_m(s + 4)
+                load_z(s + 4)
+                if s <= last + 1:
+                    finish(s - 2)
+                write_scalar(s)
+                add_write(s - 1)
+                quantize(m_grp.get(s), m_q, s, "m")
+                if s < last:
+                    quantize(z_grp.get(s), z_q, s, "z")
+                transition(s)
+                turn_m(s + 1)
+                turn_z(s + 1)
+                scale_m(s + 2)
+                if s == last + 1:
+                    quantize(z_grp.get(last), z_q, last, "z")
+                    quantize(n_grp.get(last), n_q, last, "n", 2)
+                    finish(last, 2)
+                else:
+                    quantize(n_grp.get(s - 1), n_q, s - 1, "n")
+
+            scale_m(0, 4)
+            for u in range(2):
+                nc.scalar.copy(
+                    at_grp[:, 256 * u : 256 * (u + 1), :].rearrange("p (q e) j -> p q e j", e=2),
+                    at_raw[:].rearrange("p j (q v e) -> p v q e j", v=2, e=2)[:, u],
+                )
+            turn_m(0)
+            scale_m(1, 4)
+            turn_z(0)
+            for w in range(2):
+                nc.scalar.copy(w_grp[:, w], w_raw[:, w].rearrange("p j h -> p h j"))
+            for u in range(2):
+                nc.scalar.copy(
+                    b_row[:, 256 * u : 256 * (u + 1)].rearrange("p (q e) -> p q e", e=2),
+                    b_raw[:].rearrange("p (q v e) -> p v q e", v=2, e=2)[:, u],
+                )
+            for i in range(1, TILES):
+                nc.scalar.copy(scale_row[:, i, :], scale_row[:, 0, :])
+            nc.vector.quantize_mx(
+                out=at_codes[:].bitcast(FP8X4), scales=at_scales[:], in_=at_grp[:].rearrange("p c j -> p (c j)")
+            )
+            step(0)
+            nc.vector.quantize_mx(
+                out=w_codes[:].bitcast(FP8X4), scales=w_scales[:], in_=w_grp[:].rearrange("p w h j -> p (w h j)")
+            )
+            for s in range(1, GROUPS + 1):
+                step(s)

@@ -17,6 +17,7 @@ N, K, C, H = 8192, 512, 512, 128
 TILES = 4
 GROUP = P * TILES
 GROUPS = N // GROUP
+UW = 64
 FLOPS = 2 * N * K * (C + H + H)
 
 
@@ -25,8 +26,8 @@ def tile_legendrememoryunitstep_t_kernel(tc, z, m_bytes, m_scale, ez, at, bvec, 
     with ExitStack() as ctx:
         keep = ctx.enter_context(tc.tile_pool(name="keep", bufs=1))
         loads = ctx.enter_context(tc.tile_pool(name="loads", bufs=4))
-        work = ctx.enter_context(tc.tile_pool(name="work", bufs=3))
-        quant = ctx.enter_context(tc.tile_pool(name="quant", bufs=3))
+        deep = ctx.enter_context(tc.tile_pool(name="deep", bufs=4))
+        short = ctx.enter_context(tc.tile_pool(name="short", bufs=3))
         turn = ctx.enter_context(tc.psum_pool(name="turn", bufs=3))
         acc_pool = ctx.enter_context(tc.psum_pool(name="acc", bufs=4))
         out_pool = ctx.enter_context(tc.psum_pool(name="outp", bufs=1))
@@ -35,210 +36,156 @@ def tile_legendrememoryunitstep_t_kernel(tc, z, m_bytes, m_scale, ez, at, bvec, 
         m_view = m_bytes.rearrange("(g n i) k -> g n i k", n=P, i=TILES)
         out_view = out.rearrange("(g n i) h -> g n i h", n=P, i=TILES)
 
-        z_rows, m_rows, m_vals, z_grp, m_grp, n_rows, n_grp = {}, {}, {}, {}, {}, {}, {}
-        z_q, m_q, n_q, accs, u_cols = {}, {}, {}, {}, {}
+        z_rows, m_rows, m_vals, m_grp, z_planes, zn_grp, n_rows = {}, {}, {}, {}, {}, {}, {}
+        m_q, zn_q, accs, u_cols = {}, {}, {}, {}
+
+        scale_row = keep.tile([P, TILES, K], F32, name="scale_row", align_bytes=64)
+        ident = keep.tile([P, P], F32, name="ident")
+        at_raw = keep.tile([P, 4, C], BF16, name="at_raw", align_bytes=64)
+        at_grp = keep.tile([P, C, 4], BF16, name="at_grp", align_bytes=64)
+        at_codes = keep.tile([P, C], U32, name="at_codes", align_bytes=64)
+        at_scales = keep.tile([P, C], U8, name="at_scales", align_bytes=64)
+        w_raw = keep.tile([P, 2, 4, H], BF16, name="w_raw", align_bytes=64)
+        w_grp = keep.tile([P, 2, H, 4], BF16, name="w_grp", align_bytes=64)
+        w_codes = keep.tile([P, 2 * H], U32, name="w_codes", align_bytes=64)
+        w_scales = keep.tile([P, 2 * H], U8, name="w_scales", align_bytes=64)
+        b_raw = keep.tile([P, C], BF16, name="b_raw", align_bytes=64)
+        b_row = keep.tile([P, C], BF16, name="b_row", align_bytes=64)
+        ez_cols = keep.tile([P, 4], BF16, name="ez_cols")
+        ez_wide = keep.tile([P, 4, UW], BF16, name="ez_wide")
 
         def load_m(g, parts=1):
-            if not 0 <= g < GROUPS:
-                return
             m_rows[g] = loads.tile([P, TILES, K], U8, name="m_rows", align_bytes=64)
             w = TILES // parts
             for q in range(parts):
                 nc.sync.dma_start(out=m_rows[g][:, w * q : w * (q + 1)], in_=m_view[g][:, w * q : w * (q + 1)])
 
         def load_z(g):
-            if not 0 <= g < GROUPS:
-                return
             z_rows[g] = loads.tile([P, TILES, K], BF16, name="z_rows", align_bytes=64)
             nc.sync.dma_start(out=z_rows[g][:], in_=z_view[g])
 
-        with tc.manual_schedule():
-            scale_row = keep.tile([P, TILES, K], F32, name="scale_row", align_bytes=64)
-            nc.scalar.dma_start(out=scale_row[:, 0, :], in_=m_scale.rearrange("o k -> (o k)").partition_broadcast(P))
-            load_m(0, 2)
-            dummy = keep.tile([P, 1], F32, name="dummy")
-            nc.vector.memset(dummy[:], 0.0)
-            nc.scalar.activation(dummy[:], dummy[:], ACT.Tanh)
-            ident = keep.tile([P, P], F32, name="ident")
-            make_identity(nc, ident[:])
-            at_raw = keep.tile([P, 4, C], BF16, name="at_raw", align_bytes=64)
-            nc.sync.dma_start(out=at_raw[:], in_=at.rearrange("(p j) c -> p j c", j=4))
-            load_m(1)
-            load_z(0)
-            w_raw = keep.tile([P, 2, 4, H], BF16, name="w_raw", align_bytes=64)
-            nc.sync.dma_start(out=w_raw[:, 0], in_=wz.rearrange("(p j) h -> p j h", j=4))
-            nc.sync.dma_start(out=w_raw[:, 1], in_=wm.rearrange("(p j) h -> p j h", j=4))
-            ez_cols = keep.tile([P, 4], BF16, name="ez_cols")
-            nc.sync.dma_start(out=ez_cols[:], in_=ez.rearrange("(p t) -> p t", t=4))
-            load_z(1)
-            b_raw = keep.tile([P, C], BF16, name="b_raw", align_bytes=64)
-            nc.sync.dma_start(out=b_raw[:], in_=bvec.partition_broadcast(P))
-            for g in (2, 3):
-                load_m(g)
-                load_z(g)
-
-            b_row = keep.tile([P, C], BF16, name="b_row", align_bytes=64)
-            at_grp = keep.tile([P, C, 4], BF16, name="at_grp", align_bytes=64)
-            w_grp = keep.tile([P, 2, H, 4], BF16, name="w_grp", align_bytes=64)
-            at_codes = keep.tile([P, C], U32, name="at_codes", align_bytes=64)
-            at_scales = keep.tile([P, C], U8, name="at_scales", align_bytes=64)
-            w_codes = keep.tile([P, 2 * H], U32, name="w_codes", align_bytes=64)
-            w_scales = keep.tile([P, 2 * H], U8, name="w_scales", align_bytes=64)
-
-            def scale_m(g, parts=1):
-                if not 0 <= g < GROUPS:
-                    return
-                m_vals[g] = work.tile([P, TILES, K], BF16, name="m_vals", align_bytes=64)
-                w = TILES // parts
-                for q in range(parts):
-                    nc.vector.tensor_tensor(
-                        out=m_vals[g][:, w * q : w * (q + 1)].rearrange("p i k -> p (i k)"),
-                        in0=m_rows[g][:, w * q : w * (q + 1)].rearrange("p i k -> p (i k)").bitcast(FP8),
-                        in1=scale_row[:, :w].rearrange("p i k -> p (i k)"),
-                        op=ALU.mult,
-                    )
-
-            def turn_pair(rows, grp, b, step):
-                bank = turn.tile([P, 2, 2, P], F32, name="bank")
-                for i in range(2):
-                    words = rows[:, 2 * b + i, :].bitcast(F32)
-                    for u in range(2):
-                        src = words[:, u::2] if step == 2 else words[:, P * u : P * (u + 1)]
-                        nc.tensor.transpose(bank[:, i, u, :], src, ident[:])
-                dst = grp[:, 2 * P * b : 2 * P * (b + 1), :].rearrange("p n t -> p (n t)").bitcast(F32)
-                nc.scalar.copy(
-                    dst.rearrange("p (i n u) -> p i n u", i=2, u=2),
-                    bank[:].rearrange("p i u n -> p i n u"),
+        def scale_m(g):
+            m_vals[g] = deep.tile([P, TILES, K], BF16, name="m_vals", align_bytes=64)
+            w = 1 if g == 0 else TILES
+            for i in range(0, TILES, w):
+                nc.vector.tensor_tensor(
+                    out=m_vals[g][:, i : i + w].rearrange("p i k -> p (i k)"),
+                    in0=m_rows[g][:, i : i + w].rearrange("p i k -> p (i k)").bitcast(FP8),
+                    in1=scale_row[:, :w].rearrange("p i k -> p (i k)"),
+                    op=ALU.mult,
                 )
 
-            def turn_m(g):
-                if not 0 <= g < GROUPS:
-                    return
-                m_grp[g] = work.tile([P, GROUP, 4], BF16, name="m_grp", align_bytes=64)
-                for b in range(2):
-                    turn_pair(m_vals[g], m_grp[g], b, 2)
+        def transpose_pair(rows, b, every_second):
+            bank = turn.tile([P, 2, 2, P], F32, name="bank")
+            for i in range(2):
+                words = rows[:, 2 * b + i, :].bitcast(F32)
+                for u in range(2):
+                    src = words[:, u::2] if every_second else words[:, P * u : P * (u + 1)]
+                    nc.tensor.transpose(bank[:, i, u, :], src, ident[:])
+            return bank
 
-            def turn_z(g):
-                if not 0 <= g < GROUPS:
-                    return
-                z_grp[g] = work.tile([P, GROUP, 4], BF16, name="z_grp", align_bytes=64)
-                for b in range(2):
-                    turn_pair(z_rows[g], z_grp[g], b, 2)
+        def words_of(grp, b):
+            flat = grp[:, 2 * P * b : 2 * P * (b + 1), :].rearrange("p n t -> p (n t)").bitcast(F32)
+            return flat.rearrange("p (i n u) -> p i n u", i=2, u=2)
 
-            def quantize(grp, table, g, tag, parts=1):
-                if not 0 <= g < GROUPS:
-                    return
-                codes = quant.tile([P, GROUP], U32, name=tag + "_codes", align_bytes=64)
-                scales = quant.tile([P, GROUP], U8, name=tag + "_scales", align_bytes=64)
-                w = GROUP // parts
-                for q in range(parts):
-                    cols = slice(w * q, w * (q + 1))
-                    nc.vector.quantize_mx(
-                        out=codes[:, cols].bitcast(FP8X4),
-                        scales=scales[:, cols],
-                        in_=grp[:, cols, :].rearrange("p n t -> p (n t)"),
-                    )
-                table[g] = (codes, scales)
+        def turn_m(g, b):
+            if b == 0:
+                m_grp[g] = deep.tile([P, GROUP, 4], BF16, name="m_grp", align_bytes=64)
+            bank = transpose_pair(m_vals[g], b, True)
+            nc.scalar.copy(words_of(m_grp[g], b), bank[:].rearrange("p i u n -> p i n u"))
 
-            def mx(dst, left, cols, right, rcols, start, stop):
-                nc.tensor.matmul_mx(
-                    out=dst,
-                    lhsT=left[0][:, cols].bitcast(FP8X4),
-                    lhsT_scale=left[1][:, cols],
-                    rhs=right[0][:, rcols].bitcast(FP8X4),
-                    rhs_scale=right[1][:, rcols],
-                    start=start,
-                    stop=stop,
+        def turn_z(g, b):
+            if b == 0:
+                z_planes[g] = deep.tile([P, 2, 2, 2, P], F32, name="z_planes", align_bytes=64)
+            bank = transpose_pair(z_rows[g], b, True)
+            nc.scalar.copy(z_planes[g][:, b], bank[:])
+
+        def interleave_z(g):
+            zn_grp[g] = deep.tile([P, 2, GROUP, 4], BF16, name="zn_grp", align_bytes=64)
+            flat = zn_grp[g][:, 0].rearrange("p n t -> p (n t)").bitcast(F32)
+            nc.scalar.copy(
+                flat.rearrange("p (i n u) -> p i n u", i=TILES, u=2),
+                z_planes[g][:].rearrange("p b i u n -> p (b i) n u"),
+            )
+
+        def write_scalar(g, b):
+            u_bank = turn.tile([P, 2, UW], F32, name="bank")
+            for i in range(2):
+                for t in range(4):
+                    plane = z_planes[g][:, b, i, t // 2, :].bitcast(BF16).rearrange("p (n e) -> p e n", e=2)[:, t % 2]
+                    nc.tensor.matmul(u_bank[:, i, :], lhsT=plane, rhs=ez_wide[:, t, :], start=(t == 0), stop=(t == 3))
+            u_cols[g, b] = short.tile([P, 2], F32, name="u_cols")
+            nc.scalar.copy(u_cols[g, b][:], u_bank[:, :, 0])
+
+        def mx(dst, left, cols, right, rcols, start, stop):
+            nc.tensor.matmul_mx(
+                out=dst,
+                lhsT=left[0][:, cols].bitcast(FP8X4),
+                lhsT_scale=left[1][:, cols],
+                rhs=right[0][:, rcols].bitcast(FP8X4),
+                rhs_scale=right[1][:, rcols],
+                start=start,
+                stop=stop,
+            )
+
+        def quantize(codes, scales, values, cuts):
+            for lo, hi in zip(cuts[:-1], cuts[1:]):
+                nc.vector.quantize_mx(
+                    out=codes[:, lo:hi].bitcast(FP8X4), scales=scales[:, lo:hi], in_=values[:, 4 * lo : 4 * hi]
                 )
 
-            def finish(g, parts=1):
-                if not 0 <= g < GROUPS:
-                    return
-                res = out_pool.tile([P, TILES, H], F32, name="res")
-                o_rows = work.tile([P, TILES, H], F32, name="o_rows", align_bytes=64)
-                w = TILES // parts
-                for q in range(parts):
-                    for i in range(w * q, w * (q + 1)):
-                        cols = slice(P * i, P * (i + 1))
-                        mx(res[:, i, :], z_q[g], cols, (w_codes, w_scales), slice(0, H), True, False)
-                        mx(res[:, i, :], n_q[g], cols, (w_codes, w_scales), slice(H, 2 * H), False, True)
-                    part = slice(w * q, w * (q + 1))
-                    nc.scalar.activation(o_rows[:, part], res[:, part], ACT.Tanh)
-                    nc.sync.dma_start(out=out_view[g][:, part], in_=o_rows[:, part])
+        def quantize_m(g):
+            if g == 0:
+                quantize(at_codes, at_scales, at_grp[:].rearrange("p c j -> p (c j)"), (0, C))
+            codes = short.tile([P, GROUP], U32, name="m_codes", align_bytes=64)
+            scales = short.tile([P, GROUP], U8, name="m_scales", align_bytes=64)
+            quantize(codes, scales, m_grp[g][:].rearrange("p n t -> p (n t)"), (0, GROUP))
+            m_q[g] = (codes, scales)
 
-            def write_scalar(g):
-                if not 0 <= g < GROUPS:
-                    return
-                u_bank = turn.tile([P, TILES], F32, name="bank")
-                for i in range(TILES):
-                    for t in range(4):
-                        nc.tensor.matmul(
-                            u_bank[:, i : i + 1],
-                            lhsT=z_grp[g][:, P * i : P * (i + 1), t],
-                            rhs=ez_cols[:, t : t + 1],
-                            start=(t == 0),
-                            stop=(t == 3),
-                        )
-                u_cols[g] = work.tile([P, TILES], F32, name="u_cols")
-                nc.scalar.copy(u_cols[g][:], u_bank[:])
+        def quantize_zn(g):
+            if g == 0:
+                quantize(w_codes, w_scales, w_grp[:].rearrange("p w h j -> p (w h j)"), (0, 2 * H))
+            codes = short.tile([P, 2 * GROUP], U32, name="zn_codes", align_bytes=64)
+            scales = short.tile([P, 2 * GROUP], U8, name="zn_scales", align_bytes=64)
+            cuts = (0, 2 * GROUP) if g < GROUPS - 1 else (0, GROUP, GROUP + 2 * P, 2 * GROUP)
+            quantize(codes, scales, zn_grp[g][:].rearrange("p h n t -> p (h n t)"), cuts)
+            zn_q[g] = (codes, scales)
 
-            def add_write(g):
-                if not 0 <= g < GROUPS:
-                    return
-                n_rows[g] = work.tile([P, TILES, C], BF16, name="n_rows", align_bytes=64)
-                n_grp[g] = work.tile([P, GROUP, 4], BF16, name="n_grp", align_bytes=64)
-                for b in range(2):
-                    for i in (2 * b, 2 * b + 1):
-                        nc.vector.scalar_tensor_tensor(
-                            out=n_rows[g][:, i, :],
-                            in0=b_row[:],
-                            scalar=u_cols[g][:, i : i + 1],
-                            in1=accs[g][i][:],
-                            op0=ALU.mult,
-                            op1=ALU.add,
-                        )
-                    turn_pair(n_rows[g], n_grp[g], b, 1)
+        def transition(g, b):
+            for i in (2 * b, 2 * b + 1):
+                accs[g, i] = acc_pool.tile([P, C], F32, name="acc")
+                mx(accs[g, i][:], m_q[g], slice(P * i, P * (i + 1)), (at_codes, at_scales), slice(0, C), True, True)
 
-            def transition(g):
-                if not 0 <= g < GROUPS:
-                    return
-                accs[g] = []
-                for i in range(TILES):
-                    acc = acc_pool.tile([P, C], F32, name="acc")
-                    mx(acc[:], m_q[g], slice(P * i, P * (i + 1)), (at_codes, at_scales), slice(0, C), True, True)
-                    accs[g].append(acc)
-
-            def step(s):
-                last = GROUPS - 1
-                load_m(s + 4)
-                load_z(s + 4)
-                if s <= last + 1:
-                    finish(s - 2)
-                write_scalar(s)
-                add_write(s - 1)
-                quantize(m_grp.get(s), m_q, s, "m")
-                if s < last:
-                    quantize(z_grp.get(s), z_q, s, "z")
-                transition(s)
-                turn_m(s + 1)
-                turn_z(s + 1)
-                scale_m(s + 2)
-                if s == last + 1:
-                    quantize(z_grp.get(last), z_q, last, "z")
-                    quantize(n_grp.get(last), n_q, last, "n", 2)
-                    finish(last, 2)
-                else:
-                    quantize(n_grp.get(s - 1), n_q, s - 1, "n")
-
-            scale_m(0, 4)
-            for u in range(2):
-                nc.scalar.copy(
-                    at_grp[:, 256 * u : 256 * (u + 1), :].rearrange("p (q e) j -> p q e j", e=2),
-                    at_raw[:].rearrange("p j (q v e) -> p v q e j", v=2, e=2)[:, u],
+        def add_write(g, b):
+            if b == 0:
+                n_rows[g] = short.tile([P, TILES, C], BF16, name="n_rows", align_bytes=64)
+            for i in (2 * b, 2 * b + 1):
+                nc.vector.scalar_tensor_tensor(
+                    out=n_rows[g][:, i, :],
+                    in0=b_row[:],
+                    scalar=u_cols[g, b][:, i % 2 : i % 2 + 1],
+                    in1=accs[g, i][:],
+                    op0=ALU.mult,
+                    op1=ALU.add,
                 )
-            turn_m(0)
-            scale_m(1, 4)
-            turn_z(0)
+
+        def turn_n(g, b):
+            bank = transpose_pair(n_rows[g], b, False)
+            nc.scalar.copy(words_of(zn_grp[g][:, 1], b), bank[:].rearrange("p i u n -> p i n u"))
+
+        def finish(g):
+            res = out_pool.tile([P, TILES, H], F32, name="res")
+            o_rows = short.tile([P, TILES, H], F32, name="o_rows", align_bytes=64)
+            w = TILES if g < GROUPS - 1 else 2
+            for q in range(0, TILES, w):
+                for i in range(q, q + w):
+                    for h in range(2):
+                        cols = slice(GROUP * h + P * i, GROUP * h + P * (i + 1))
+                        mx(res[:, i, :], zn_q[g], cols, (w_codes, w_scales), slice(H * h, H * (h + 1)), h == 0, h == 1)
+                nc.scalar.activation(o_rows[:, q : q + w], res[:, q : q + w], ACT.Tanh)
+                nc.sync.dma_start(out=out_view[g][:, q : q + w], in_=o_rows[:, q : q + w])
+
+        def interleave_small():
             for w in range(2):
                 nc.scalar.copy(w_grp[:, w], w_raw[:, w].rearrange("p j h -> p h j"))
             for u in range(2):
@@ -246,14 +193,59 @@ def tile_legendrememoryunitstep_t_kernel(tc, z, m_bytes, m_scale, ez, at, bvec, 
                     b_row[:, 256 * u : 256 * (u + 1)].rearrange("p (q e) -> p q e", e=2),
                     b_raw[:].rearrange("p (q v e) -> p v q e", v=2, e=2)[:, u],
                 )
+
+        with tc.manual_schedule():
+            nc.scalar.dma_start(out=scale_row[:, 0, :], in_=m_scale.rearrange("o k -> (o k)").partition_broadcast(P))
+            load_m(0, 2)
+            dummy = keep.tile([P, 1], F32, name="dummy")
+            nc.vector.memset(dummy[:], 0.0)
+            nc.scalar.activation(dummy[:], dummy[:], ACT.Tanh)
+            make_identity(nc, ident[:])
+            nc.sync.dma_start(out=at_raw[:], in_=at.rearrange("(p j) c -> p j c", j=4))
+            load_m(1)
+            load_z(0)
+            load_m(2)
+            nc.sync.dma_start(out=ez_cols[:], in_=ez.rearrange("(p t) -> p t", t=4))
+            nc.sync.dma_start(out=w_raw[:, 0], in_=wz.rearrange("(p j) h -> p j h", j=4))
+            nc.sync.dma_start(out=w_raw[:, 1], in_=wm.rearrange("(p j) h -> p j h", j=4))
+            load_z(1)
+            load_m(3)
+            nc.sync.dma_start(out=b_raw[:], in_=bvec.partition_broadcast(P))
+            nc.gpsimd.tensor_copy(out=ez_wide[:], in_=ez_cols[:].unsqueeze(2).to_broadcast([P, 4, UW]))
             for i in range(1, TILES):
                 nc.scalar.copy(scale_row[:, i, :], scale_row[:, 0, :])
-            nc.vector.quantize_mx(
-                out=at_codes[:].bitcast(FP8X4), scales=at_scales[:], in_=at_grp[:].rearrange("p c j -> p (c j)")
+            for u in range(2):
+                nc.scalar.copy(
+                    at_grp[:, 256 * u : 256 * (u + 1), :].rearrange("p (q e) j -> p q e j", e=2),
+                    at_raw[:].rearrange("p j (q v e) -> p v q e j", v=2, e=2)[:, u],
+                )
+
+            stages = (
+                (load_m, 6, ()),
+                (load_z, 4, ()),
+                (turn_m, 2, (0,)),
+                (turn_m, 2, (1,)),
+                (turn_z, 2, (0,)),
+                (write_scalar, 0, (0,)),
+                (interleave_z, 0, ()),
+                (quantize_m, 0, ()),
+                (add_write, -1, (0,)),
+                (transition, 0, (0,)),
+                (write_scalar, 0, (1,)),
+                (turn_z, 2, (1,)),
+                (add_write, -1, (1,)),
+                (quantize_zn, -2, ()),
+                (turn_n, -1, (0,)),
+                (turn_n, -1, (1,)),
+                (scale_m, 4, ()),
+                (transition, 0, (1,)),
+                (finish, -2, ()),
             )
-            step(0)
-            nc.vector.quantize_mx(
-                out=w_codes[:].bitcast(FP8X4), scales=w_scales[:], in_=w_grp[:].rearrange("p w h j -> p (w h j)")
-            )
-            for s in range(1, GROUPS + 1):
-                step(s)
+            for s in range(-4, GROUPS + 2):
+                if s == -1:
+                    interleave_small()
+                for stage, ahead, half in stages:
+                    g = s + ahead
+                    preloaded = (stage is load_m and g < 4) or (stage is load_z and g < 2)
+                    if 0 <= g < GROUPS and not preloaded:
+                        stage(g, *half)

from contextlib import ExitStack

import concourse.mybir as mybir
from concourse.masks import make_identity

F32 = mybir.dt.float32
BF16 = mybir.dt.bfloat16
U32 = mybir.dt.uint32
U8 = mybir.dt.uint8
FP8 = mybir.dt.float8_e4m3fn
FP8X4 = mybir.dt.float8_e4m3fn_x4
ALU = mybir.AluOpType
ACT = mybir.ActivationFunctionType

P = 128
N, K, C, H = 8192, 512, 512, 128
TILES = 4
GROUP = P * TILES
GROUPS = N // GROUP
UW = 64
FLOPS = 2 * N * K * (C + H + H)


def tile_legendrememoryunitstep_t_kernel(tc, z, m_bytes, m_scale, ez, at, bvec, wz, wm, out):
    nc = tc.nc
    with ExitStack() as ctx:
        keep = ctx.enter_context(tc.tile_pool(name="keep", bufs=1))
        loads = ctx.enter_context(tc.tile_pool(name="loads", bufs=4))
        deep = ctx.enter_context(tc.tile_pool(name="deep", bufs=4))
        short = ctx.enter_context(tc.tile_pool(name="short", bufs=3))
        turn = ctx.enter_context(tc.psum_pool(name="turn", bufs=3))
        acc_pool = ctx.enter_context(tc.psum_pool(name="acc", bufs=4))
        out_pool = ctx.enter_context(tc.psum_pool(name="outp", bufs=1))

        z_view = z.rearrange("(g n i) k -> g n i k", n=P, i=TILES)
        m_view = m_bytes.rearrange("(g n i) k -> g n i k", n=P, i=TILES)
        out_view = out.rearrange("(g n i) h -> g n i h", n=P, i=TILES)

        z_rows, m_rows, m_vals, m_grp, z_planes, zn_grp, n_rows = {}, {}, {}, {}, {}, {}, {}
        m_q, zn_q, accs, u_cols = {}, {}, {}, {}

        scale_row = keep.tile([P, TILES, K], F32, name="scale_row", align_bytes=64)
        ident = keep.tile([P, P], F32, name="ident")
        at_raw = keep.tile([P, 4, C], BF16, name="at_raw", align_bytes=64)
        at_grp = keep.tile([P, C, 4], BF16, name="at_grp", align_bytes=64)
        at_codes = keep.tile([P, C], U32, name="at_codes", align_bytes=64)
        at_scales = keep.tile([P, C], U8, name="at_scales", align_bytes=64)
        w_raw = keep.tile([P, 2, 4, H], BF16, name="w_raw", align_bytes=64)
        w_grp = keep.tile([P, 2, H, 4], BF16, name="w_grp", align_bytes=64)
        w_codes = keep.tile([P, 2 * H], U32, name="w_codes", align_bytes=64)
        w_scales = keep.tile([P, 2 * H], U8, name="w_scales", align_bytes=64)
        b_raw = keep.tile([P, C], BF16, name="b_raw", align_bytes=64)
        b_row = keep.tile([P, C], BF16, name="b_row", align_bytes=64)
        ez_cols = keep.tile([P, 4], BF16, name="ez_cols")
        ez_wide = keep.tile([P, 4, UW], BF16, name="ez_wide")

        def load_m(g, parts=1):
            m_rows[g] = loads.tile([P, TILES, K], U8, name="m_rows", align_bytes=64)
            w = TILES // parts
            for q in range(parts):
                nc.sync.dma_start(out=m_rows[g][:, w * q : w * (q + 1)], in_=m_view[g][:, w * q : w * (q + 1)])

        def load_z(g):
            z_rows[g] = loads.tile([P, TILES, K], BF16, name="z_rows", align_bytes=64)
            nc.sync.dma_start(out=z_rows[g][:], in_=z_view[g])

        def scale_m(g):
            m_vals[g] = deep.tile([P, TILES, K], BF16, name="m_vals", align_bytes=64)
            w = 1 if g == 0 else TILES
            for i in range(0, TILES, w):
                nc.vector.tensor_tensor(
                    out=m_vals[g][:, i : i + w].rearrange("p i k -> p (i k)"),
                    in0=m_rows[g][:, i : i + w].rearrange("p i k -> p (i k)").bitcast(FP8),
                    in1=scale_row[:, :w].rearrange("p i k -> p (i k)"),
                    op=ALU.mult,
                )

        def transpose_pair(rows, b, every_second):
            bank = turn.tile([P, 2, 2, P], F32, name="bank")
            for i in range(2):
                words = rows[:, 2 * b + i, :].bitcast(F32)
                for u in range(2):
                    src = words[:, u::2] if every_second else words[:, P * u : P * (u + 1)]
                    nc.tensor.transpose(bank[:, i, u, :], src, ident[:])
            return bank

        def words_of(grp, b):
            flat = grp[:, 2 * P * b : 2 * P * (b + 1), :].rearrange("p n t -> p (n t)").bitcast(F32)
            return flat.rearrange("p (i n u) -> p i n u", i=2, u=2)

        def turn_m(g, b):
            if b == 0:
                m_grp[g] = deep.tile([P, GROUP, 4], BF16, name="m_grp", align_bytes=64)
            bank = transpose_pair(m_vals[g], b, True)
            nc.scalar.copy(words_of(m_grp[g], b), bank[:].rearrange("p i u n -> p i n u"))

        def turn_z(g, b):
            if b == 0:
                z_planes[g] = deep.tile([P, 2, 2, 2, P], F32, name="z_planes", align_bytes=64)
            bank = transpose_pair(z_rows[g], b, True)
            nc.scalar.copy(z_planes[g][:, b], bank[:])

        def interleave_z(g):
            zn_grp[g] = deep.tile([P, 2, GROUP, 4], BF16, name="zn_grp", align_bytes=64)
            flat = zn_grp[g][:, 0].rearrange("p n t -> p (n t)").bitcast(F32)
            nc.scalar.copy(
                flat.rearrange("p (i n u) -> p i n u", i=TILES, u=2),
                z_planes[g][:].rearrange("p b i u n -> p (b i) n u"),
            )

        def write_scalar(g, b):
            u_bank = turn.tile([P, 2, UW], F32, name="bank")
            for i in range(2):
                for t in range(4):
                    plane = z_planes[g][:, b, i, t // 2, :].bitcast(BF16).rearrange("p (n e) -> p e n", e=2)[:, t % 2]
                    nc.tensor.matmul(u_bank[:, i, :], lhsT=plane, rhs=ez_wide[:, t, :], start=(t == 0), stop=(t == 3))
            u_cols[g, b] = short.tile([P, 2], F32, name="u_cols")
            nc.scalar.copy(u_cols[g, b][:], u_bank[:, :, 0])

        def mx(dst, left, cols, right, rcols, start, stop):
            nc.tensor.matmul_mx(
                out=dst,
                lhsT=left[0][:, cols].bitcast(FP8X4),
                lhsT_scale=left[1][:, cols],
                rhs=right[0][:, rcols].bitcast(FP8X4),
                rhs_scale=right[1][:, rcols],
                start=start,
                stop=stop,
            )

        def quantize(codes, scales, values, cuts):
            for lo, hi in zip(cuts[:-1], cuts[1:]):
                nc.vector.quantize_mx(
                    out=codes[:, lo:hi].bitcast(FP8X4), scales=scales[:, lo:hi], in_=values[:, 4 * lo : 4 * hi]
                )

        def quantize_m(g):
            if g == 0:
                quantize(at_codes, at_scales, at_grp[:].rearrange("p c j -> p (c j)"), (0, C))
            codes = short.tile([P, GROUP], U32, name="m_codes", align_bytes=64)
            scales = short.tile([P, GROUP], U8, name="m_scales", align_bytes=64)
            quantize(codes, scales, m_grp[g][:].rearrange("p n t -> p (n t)"), (0, GROUP))
            m_q[g] = (codes, scales)

        def quantize_zn(g):
            if g == 0:
                quantize(w_codes, w_scales, w_grp[:].rearrange("p w h j -> p (w h j)"), (0, 2 * H))
            codes = short.tile([P, 2 * GROUP], U32, name="zn_codes", align_bytes=64)
            scales = short.tile([P, 2 * GROUP], U8, name="zn_scales", align_bytes=64)
            cuts = (0, 2 * GROUP) if g < GROUPS - 1 else (0, GROUP, GROUP + 2 * P, 2 * GROUP)
            quantize(codes, scales, zn_grp[g][:].rearrange("p h n t -> p (h n t)"), cuts)
            zn_q[g] = (codes, scales)

        def transition(g, b):
            for i in (2 * b, 2 * b + 1):
                accs[g, i] = acc_pool.tile([P, C], F32, name="acc")
                mx(accs[g, i][:], m_q[g], slice(P * i, P * (i + 1)), (at_codes, at_scales), slice(0, C), True, True)

        def add_write(g, b):
            if b == 0:
                n_rows[g] = short.tile([P, TILES, C], BF16, name="n_rows", align_bytes=64)
            for i in (2 * b, 2 * b + 1):
                nc.vector.scalar_tensor_tensor(
                    out=n_rows[g][:, i, :],
                    in0=b_row[:],
                    scalar=u_cols[g, b][:, i % 2 : i % 2 + 1],
                    in1=accs[g, i][:],
                    op0=ALU.mult,
                    op1=ALU.add,
                )

        def turn_n(g, b):
            bank = transpose_pair(n_rows[g], b, False)
            nc.scalar.copy(words_of(zn_grp[g][:, 1], b), bank[:].rearrange("p i u n -> p i n u"))

        def finish(g):
            res = out_pool.tile([P, TILES, H], F32, name="res")
            o_rows = short.tile([P, TILES, H], F32, name="o_rows", align_bytes=64)
            w = TILES if g < GROUPS - 1 else 2
            for q in range(0, TILES, w):
                for i in range(q, q + w):
                    for h in range(2):
                        cols = slice(GROUP * h + P * i, GROUP * h + P * (i + 1))
                        mx(res[:, i, :], zn_q[g], cols, (w_codes, w_scales), slice(H * h, H * (h + 1)), h == 0, h == 1)
                nc.scalar.activation(o_rows[:, q : q + w], res[:, q : q + w], ACT.Tanh)
                nc.sync.dma_start(out=out_view[g][:, q : q + w], in_=o_rows[:, q : q + w])

        def interleave_small():
            for w in range(2):
                nc.scalar.copy(w_grp[:, w], w_raw[:, w].rearrange("p j h -> p h j"))
            for u in range(2):
                nc.scalar.copy(
                    b_row[:, 256 * u : 256 * (u + 1)].rearrange("p (q e) -> p q e", e=2),
                    b_raw[:].rearrange("p (q v e) -> p v q e", v=2, e=2)[:, u],
                )

        with tc.manual_schedule():
            nc.scalar.dma_start(out=scale_row[:, 0, :], in_=m_scale.rearrange("o k -> (o k)").partition_broadcast(P))
            load_m(0, 2)
            dummy = keep.tile([P, 1], F32, name="dummy")
            nc.vector.memset(dummy[:], 0.0)
            nc.scalar.activation(dummy[:], dummy[:], ACT.Tanh)
            make_identity(nc, ident[:])
            nc.sync.dma_start(out=at_raw[:], in_=at.rearrange("(p j) c -> p j c", j=4))
            load_m(1)
            load_z(0)
            load_m(2)
            nc.sync.dma_start(out=ez_cols[:], in_=ez.rearrange("(p t) -> p t", t=4))
            nc.sync.dma_start(out=w_raw[:, 0], in_=wz.rearrange("(p j) h -> p j h", j=4))
            nc.sync.dma_start(out=w_raw[:, 1], in_=wm.rearrange("(p j) h -> p j h", j=4))
            load_z(1)
            load_m(3)
            nc.sync.dma_start(out=b_raw[:], in_=bvec.partition_broadcast(P))
            nc.gpsimd.tensor_copy(out=ez_wide[:], in_=ez_cols[:].unsqueeze(2).to_broadcast([P, 4, UW]))
            for i in range(1, TILES):
                nc.scalar.copy(scale_row[:, i, :], scale_row[:, 0, :])
            for u in range(2):
                nc.scalar.copy(
                    at_grp[:, 256 * u : 256 * (u + 1), :].rearrange("p (q e) j -> p q e j", e=2),
                    at_raw[:].rearrange("p j (q v e) -> p v q e j", v=2, e=2)[:, u],
                )

            stages = (
                (load_m, 6, ()),
                (load_z, 4, ()),
                (turn_m, 2, (0,)),
                (turn_m, 2, (1,)),
                (turn_z, 2, (0,)),
                (write_scalar, 0, (0,)),
                (interleave_z, 0, ()),
                (quantize_m, 0, ()),
                (add_write, -1, (0,)),
                (transition, 0, (0,)),
                (write_scalar, 0, (1,)),
                (turn_z, 2, (1,)),
                (add_write, -1, (1,)),
                (quantize_zn, -2, ()),
                (turn_n, -1, (0,)),
                (turn_n, -1, (1,)),
                (scale_m, 4, ()),
                (transition, 0, (1,)),
                (finish, -2, ()),
            )
            for s in range(-4, GROUPS + 2):
                if s == -1:
                    interleave_small()
                for stage, ahead, half in stages:
                    g = s + ahead
                    preloaded = (stage is load_m and g < 4) or (stage is load_z and g < 2)
                    if 0 <= g < GROUPS and not preloaded:
                        stage(g, *half)
